import numpy as np
import ml_dtypes

BF16 = ml_dtypes.bfloat16


def bf(x):
    return np.asarray(x, np.float32).astype(BF16)


def f32(x):
    return np.asarray(x, np.float32)


def f64(x):
    return np.asarray(x).astype(np.float64)


def striped(idx):
    return np.tile(idx.reshape(-1, 16).T, (8, 1))


S, K, M, N, B, Q = 512, 128, 256, 512, 2, 256


def setup_inputs():
    return {"base": bf(np.random.standard_normal((B, M, S))), "x": bf(np.random.standard_normal((K, N))), "w": bf(np.random.standard_normal((K, M)) / np.sqrt(K)), "offs": striped(np.random.permutation(S))}


def reference(base, x, w, offs):
    idx = offs[:16].T.reshape(-1)
    z = f64(base).copy()
    for i in range(B):
        z[i][:, idx[i * Q : (i + 1) * Q]] = f64(w).T @ f64(x)[:, i * Q : (i + 1) * Q]
    return z

@@ -1,0 +1,62 @@
+import concourse.mybir as mybir
+from concourse.masks import make_identity
+
+BF16, F32, U16 = mybir.dt.bfloat16, mybir.dt.float32, mybir.dt.uint16
+
+P = 128
+SEQS = 2
+BLOCKS = 2
+TOKENS = 512
+PIECE = 256
+PIECE_COLS = PIECE // 16
+
+FLOPS = 2 * P * (BLOCKS * P) * (SEQS * PIECE)
+
+
+def tile_scatter_matmul_kernel(tc, base, x, w, offs, out):
+    nc = tc.nc
+    pairs = [(i, a) for i in range(SEQS) for a in range(BLOCKS)]
+
+    with (
+        tc.tile_pool(name="held", bufs=1) as held,
+        tc.psum_pool(name="banks", bufs=1) as banks,
+    ):
+        offsets = held.tile([P, SEQS * PIECE_COLS], U16, name="offsets")
+        nc.sync.dma_start(offsets[:], offs)
+
+        ident = held.tile([P, P], BF16, name="ident")
+        make_identity(nc, ident[:])
+
+        base_tiles = {}
+        for n, (i, a) in enumerate(pairs):
+            base_tiles[i, a] = held.tile([P, TOKENS], BF16, name="base_%d_%d" % (i, a))
+            queue = nc.sync if n % 2 == 0 else nc.scalar
+            queue.dma_start(base_tiles[i, a][:], base[i, a * P : (a + 1) * P, :])
+
+        w_tile = held.tile([P, BLOCKS * P], BF16, name="w_tile")
+        nc.gpsimd.dma_start(w_tile[:], w)
+        x_tile = held.tile([P, SEQS * PIECE], BF16, name="x_tile")
+        nc.gpsimd.dma_start(x_tile[:], x)
+
+        windows = {}
+        for i, a in pairs:
+            windows[i, a] = banks.tile([P, TOKENS], F32, name="window_%d_%d" % (i, a))
+            nc.tensor.matmul(windows[i, a][:], ident[:], base_tiles[i, a][:], start=True, stop=True)
+
+        for i, a in pairs:
+            nc.tensor.matmul(
+                windows[i, a][:].indirect(offsets[:, i * PIECE_COLS : (i + 1) * PIECE_COLS]),
+                w_tile[:, a * P : (a + 1) * P],
+                x_tile[:, i * PIECE : (i + 1) * PIECE],
+                start=True,
+                stop=True,
+            )
+
+        for n, (i, a) in enumerate(pairs):
+            staged = held.tile([P, TOKENS], F32, name="staged_%d_%d" % (i, a))
+            if n % 2 == 0:
+                nc.vector.tensor_copy(staged[:], windows[i, a][:])
+                nc.sync.dma_start(out[i, a * P : (a + 1) * P, :], staged[:])
+            else:
+                nc.scalar.copy(staged[:], windows[i, a][:])
+                nc.scalar.dma_start(out[i, a * P : (a + 1) * P, :], staged[:])

@@ -21,9 +21,6 @@ def tile_scatter_matmul_kernel(tc, base, x, w, offs, out):
         tc.tile_pool(name="held", bufs=1) as held,
         tc.psum_pool(name="banks", bufs=1) as banks,
     ):
-        offsets = held.tile([P, SEQS * PIECE_COLS], U16, name="offsets")
-        nc.sync.dma_start(offsets[:], offs)
-
         ident = held.tile([P, P], BF16, name="ident")
         make_identity(nc, ident[:])
 
@@ -33,10 +30,12 @@ def tile_scatter_matmul_kernel(tc, base, x, w, offs, out):
             queue = nc.sync if n % 2 == 0 else nc.scalar
             queue.dma_start(base_tiles[i, a][:], base[i, a * P : (a + 1) * P, :])
 
+        offsets = held.tile([P, SEQS * PIECE_COLS], U16, name="offsets")
+        nc.sync.dma_start(offsets[:], offs)
         w_tile = held.tile([P, BLOCKS * P], BF16, name="w_tile")
-        nc.gpsimd.dma_start(w_tile[:], w)
+        nc.scalar.dma_start(w_tile[:], w)
         x_tile = held.tile([P, SEQS * PIECE], BF16, name="x_tile")
-        nc.gpsimd.dma_start(x_tile[:], x)
+        nc.sync.dma_start(x_tile[:], x)
 
         windows = {}
         for i, a in pairs:

@@ -9,6 +9,7 @@ BLOCKS = 2
 TOKENS = 512
 PIECE = 256
 PIECE_COLS = PIECE // 16
+WARM_UPS = 4
 
 FLOPS = 2 * P * (BLOCKS * P) * (SEQS * PIECE)
 
@@ -21,6 +22,12 @@ def tile_scatter_matmul_kernel(tc, base, x, w, offs, out):
         tc.tile_pool(name="held", bufs=1) as held,
         tc.psum_pool(name="banks", bufs=1) as banks,
     ):
+        zeros = held.tile([P, TOKENS], BF16, name="zeros")
+        nc.vector.memset(zeros[:], 0.0)
+        unused = banks.tile([P, TOKENS], F32, name="unused")
+        for n in range(WARM_UPS):
+            nc.tensor.matmul(unused[:], zeros[:, 0:P], zeros[:], start=True, stop=True)
+
         ident = held.tile([P, P], BF16, name="ident")
         make_identity(nc, ident[:])
 

@@ -7,6 +7,7 @@ P = 128
 SEQS = 2
 BLOCKS = 2
 TOKENS = 512
+HALF = TOKENS // 2
 PIECE = 256
 PIECE_COLS = PIECE // 16
 WARM_UPS = 4
@@ -59,10 +60,12 @@ def tile_scatter_matmul_kernel(tc, base, x, w, offs, out):
             )
 
         for n, (i, a) in enumerate(pairs):
-            staged = held.tile([P, TOKENS], F32, name="staged_%d_%d" % (i, a))
-            if n % 2 == 0:
-                nc.vector.tensor_copy(staged[:], windows[i, a][:])
-                nc.sync.dma_start(out[i, a * P : (a + 1) * P, :], staged[:])
-            else:
-                nc.scalar.copy(staged[:], windows[i, a][:])
-                nc.scalar.dma_start(out[i, a * P : (a + 1) * P, :], staged[:])
+            for h in range(2):
+                cols = slice(h * HALF, (h + 1) * HALF)
+                staged = held.tile([P, HALF], F32, name="staged_%d_%d_%d" % (i, a, h))
+                if n % 2 == 0:
+                    nc.vector.tensor_copy(staged[:], windows[i, a][:, cols])
+                    nc.sync.dma_start(out[i, a * P : (a + 1) * P, cols], staged[:])
+                else:
+                    nc.scalar.copy(staged[:], windows[i, a][:, cols])
+                    nc.scalar.dma_start(out[i, a * P : (a + 1) * P, cols], staged[:])

@@ -11,13 +11,16 @@ HALF = TOKENS // 2
 PIECE = 256
 PIECE_COLS = PIECE // 16
 WARM_UPS = 4
+BETWEEN_RUNS = 24
+FILL = 64
+FILLS = BLOCKS * TOKENS // FILL
+SPACERS = BETWEEN_RUNS - FILLS
 
 FLOPS = 2 * P * (BLOCKS * P) * (SEQS * PIECE)
 
 
 def tile_scatter_matmul_kernel(tc, base, x, w, offs, out):
     nc = tc.nc
-    pairs = [(i, a) for i in range(SEQS) for a in range(BLOCKS)]
 
     with (
         tc.tile_pool(name="held", bufs=1) as held,
@@ -33,39 +36,58 @@ def tile_scatter_matmul_kernel(tc, base, x, w, offs, out):
         make_identity(nc, ident[:])
 
         base_tiles = {}
-        for n, (i, a) in enumerate(pairs):
-            base_tiles[i, a] = held.tile([P, TOKENS], BF16, name="base_%d_%d" % (i, a))
-            queue = nc.sync if n % 2 == 0 else nc.scalar
-            queue.dma_start(base_tiles[i, a][:], base[i, a * P : (a + 1) * P, :])
-
+        x_tiles = {}
+        for i in range(SEQS):
+            for a in range(BLOCKS):
+                base_tiles[i, a] = held.tile([P, TOKENS], BF16, name="base_%d_%d" % (i, a))
+            x_tiles[i] = held.tile([P, PIECE], BF16, name="x_%d" % i)
         offsets = held.tile([P, SEQS * PIECE_COLS], U16, name="offsets")
-        nc.sync.dma_start(offsets[:], offs)
         w_tile = held.tile([P, BLOCKS * P], BF16, name="w_tile")
+
+        nc.sync.dma_start(base_tiles[0, 0][:], base[0, 0:P, :])
+        nc.scalar.dma_start(base_tiles[0, 1][:], base[0, P : 2 * P, :])
+        nc.sync.dma_start(offsets[:], offs)
         nc.scalar.dma_start(w_tile[:], w)
-        x_tile = held.tile([P, SEQS * PIECE], BF16, name="x_tile")
-        nc.sync.dma_start(x_tile[:], x)
+        nc.sync.dma_start(x_tiles[0][:], x[:, 0:PIECE])
+        nc.sync.dma_start(base_tiles[1, 0][:], base[1, 0:P, :])
+        nc.scalar.dma_start(base_tiles[1, 1][:], base[1, P : 2 * P, :])
+        nc.scalar.dma_start(x_tiles[1][:], x[:, PIECE : 2 * PIECE])
 
         windows = {}
-        for i, a in pairs:
-            windows[i, a] = banks.tile([P, TOKENS], F32, name="window_%d_%d" % (i, a))
-            nc.tensor.matmul(windows[i, a][:], ident[:], base_tiles[i, a][:], start=True, stop=True)
+        for i in range(SEQS):
+            if i > 0:
+                for n in range(SPACERS):
+                    nc.tensor.matmul(
+                        unused[:, 0:FILL], ident[:], base_tiles[i, 0][:, 0:FILL], start=True, stop=True
+                    )
 
-        for i, a in pairs:
-            nc.tensor.matmul(
-                windows[i, a][:].indirect(offsets[:, i * PIECE_COLS : (i + 1) * PIECE_COLS]),
-                w_tile[:, a * P : (a + 1) * P],
-                x_tile[:, i * PIECE : (i + 1) * PIECE],
-                start=True,
-                stop=True,
-            )
+            for a in range(BLOCKS):
+                windows[i, a] = banks.tile([P, TOKENS], F32, name="window_%d_%d" % (i, a))
+                for c in range(0, TOKENS, FILL):
+                    nc.tensor.matmul(
+                        windows[i, a][:, c : c + FILL],
+                        ident[:],
+                        base_tiles[i, a][:, c : c + FILL],
+                        start=True,
+                        stop=True,
+                    )
 
-        for n, (i, a) in enumerate(pairs):
-            for h in range(2):
-                cols = slice(h * HALF, (h + 1) * HALF)
-                staged = held.tile([P, HALF], F32, name="staged_%d_%d_%d" % (i, a, h))
-                if n % 2 == 0:
-                    nc.vector.tensor_copy(staged[:], windows[i, a][:, cols])
-                    nc.sync.dma_start(out[i, a * P : (a + 1) * P, cols], staged[:])
-                else:
-                    nc.scalar.copy(staged[:], windows[i, a][:, cols])
-                    nc.scalar.dma_start(out[i, a * P : (a + 1) * P, cols], staged[:])
+            for a in range(BLOCKS):
+                nc.tensor.matmul(
+                    windows[i, a][:].indirect(offsets[:, i * PIECE_COLS : (i + 1) * PIECE_COLS]),
+                    w_tile[:, a * P : (a + 1) * P],
+                    x_tiles[i][:],
+                    start=True,
+                    stop=True,
+                )
+
+            for a in range(BLOCKS):
+                for h in range(2):
+                    cols = slice(h * HALF, (h + 1) * HALF)
+                    staged = held.tile([P, HALF], F32, name="staged_%d_%d_%d" % (i, a, h))
+                    if a == 0:
+                        nc.vector.tensor_copy(staged[:], windows[i, a][:, cols])
+                        nc.sync.dma_start(out[i, a * P : (a + 1) * P, cols], staged[:])
+                    else:
+                        nc.scalar.copy(staged[:], windows[i, a][:, cols])
+                        nc.scalar.dma_start(out[i, a * P : (a + 1) * P, cols], staged[:])

@@ -10,7 +10,7 @@ TOKENS = 512
 HALF = TOKENS // 2
 PIECE = 256
 PIECE_COLS = PIECE // 16
-WARM_UPS = 4
+WARM_UPS = 2
 BETWEEN_RUNS = 24
 FILL = 64
 FILLS = BLOCKS * TOKENS // FILL

@@ -11,16 +11,14 @@ HALF = TOKENS // 2
 PIECE = 256
 PIECE_COLS = PIECE // 16
 WARM_UPS = 2
-BETWEEN_RUNS = 24
 FILL = 64
-FILLS = BLOCKS * TOKENS // FILL
-SPACERS = BETWEEN_RUNS - FILLS
 
 FLOPS = 2 * P * (BLOCKS * P) * (SEQS * PIECE)
 
 
 def tile_scatter_matmul_kernel(tc, base, x, w, offs, out):
     nc = tc.nc
+    pairs = [(i, a) for i in range(SEQS) for a in range(BLOCKS)]
 
     with (
         tc.tile_pool(name="held", bufs=1) as held,
@@ -37,57 +35,64 @@ def tile_scatter_matmul_kernel(tc, base, x, w, offs, out):
 
         base_tiles = {}
         x_tiles = {}
+        for i, a in pairs:
+            base_tiles[i, a] = held.tile([P, TOKENS], BF16, name="base_%d_%d" % (i, a))
         for i in range(SEQS):
-            for a in range(BLOCKS):
-                base_tiles[i, a] = held.tile([P, TOKENS], BF16, name="base_%d_%d" % (i, a))
             x_tiles[i] = held.tile([P, PIECE], BF16, name="x_%d" % i)
         offsets = held.tile([P, SEQS * PIECE_COLS], U16, name="offsets")
         w_tile = held.tile([P, BLOCKS * P], BF16, name="w_tile")
 
         nc.sync.dma_start(base_tiles[0, 0][:], base[0, 0:P, :])
-        nc.scalar.dma_start(base_tiles[0, 1][:], base[0, P : 2 * P, :])
-        nc.sync.dma_start(offsets[:], offs)
         nc.scalar.dma_start(w_tile[:], w)
-        nc.sync.dma_start(x_tiles[0][:], x[:, 0:PIECE])
-        nc.sync.dma_start(base_tiles[1, 0][:], base[1, 0:P, :])
-        nc.scalar.dma_start(base_tiles[1, 1][:], base[1, P : 2 * P, :])
+        nc.sync.dma_start(offsets[:], offs)
+        nc.scalar.dma_start(x_tiles[0][:], x[:, 0:PIECE])
+        nc.sync.dma_start(base_tiles[0, 1][:], base[0, P : 2 * P, :])
+        nc.scalar.dma_start(base_tiles[1, 0][:], base[1, 0:P, :])
+        nc.sync.dma_start(base_tiles[1, 1][:], base[1, P : 2 * P, :])
         nc.scalar.dma_start(x_tiles[1][:], x[:, PIECE : 2 * PIECE])
 
         windows = {}
-        for i in range(SEQS):
-            if i > 0:
-                for n in range(SPACERS):
-                    nc.tensor.matmul(
-                        unused[:, 0:FILL], ident[:], base_tiles[i, 0][:, 0:FILL], start=True, stop=True
-                    )
+        for i, a in pairs:
+            windows[i, a] = banks.tile([P, TOKENS], F32, name="window_%d_%d" % (i, a))
 
-            for a in range(BLOCKS):
-                windows[i, a] = banks.tile([P, TOKENS], F32, name="window_%d_%d" % (i, a))
-                for c in range(0, TOKENS, FILL):
-                    nc.tensor.matmul(
-                        windows[i, a][:, c : c + FILL],
-                        ident[:],
-                        base_tiles[i, a][:, c : c + FILL],
-                        start=True,
-                        stop=True,
-                    )
-
-            for a in range(BLOCKS):
+        def fill(i, a):
+            for c in range(0, TOKENS, FILL):
                 nc.tensor.matmul(
-                    windows[i, a][:].indirect(offsets[:, i * PIECE_COLS : (i + 1) * PIECE_COLS]),
-                    w_tile[:, a * P : (a + 1) * P],
-                    x_tiles[i][:],
+                    windows[i, a][:, c : c + FILL],
+                    ident[:],
+                    base_tiles[i, a][:, c : c + FILL],
                     start=True,
                     stop=True,
                 )
 
-            for a in range(BLOCKS):
-                for h in range(2):
-                    cols = slice(h * HALF, (h + 1) * HALF)
-                    staged = held.tile([P, HALF], F32, name="staged_%d_%d_%d" % (i, a, h))
-                    if a == 0:
-                        nc.vector.tensor_copy(staged[:], windows[i, a][:, cols])
-                        nc.sync.dma_start(out[i, a * P : (a + 1) * P, cols], staged[:])
-                    else:
-                        nc.scalar.copy(staged[:], windows[i, a][:, cols])
-                        nc.scalar.dma_start(out[i, a * P : (a + 1) * P, cols], staged[:])
+        def scatter(i, a):
+            nc.tensor.matmul(
+                windows[i, a][:].indirect(offsets[:, i * PIECE_COLS : (i + 1) * PIECE_COLS]),
+                w_tile[:, a * P : (a + 1) * P],
+                x_tiles[i][:],
+                start=True,
+                stop=True,
+            )
+
+        def copy_and_store(n, i, a):
+            for h in range(2):
+                cols = slice(h * HALF, (h + 1) * HALF)
+                staged = held.tile([P, HALF], F32, name="staged_%d_%d_%d" % (i, a, h))
+                if n % 2 == 0:
+                    nc.vector.tensor_copy(staged[:], windows[i, a][:, cols])
+                    nc.sync.dma_start(out[i, a * P : (a + 1) * P, cols], staged[:])
+                else:
+                    nc.scalar.copy(staged[:], windows[i, a][:, cols])
+                    nc.scalar.dma_start(out[i, a * P : (a + 1) * P, cols], staged[:])
+
+        fill(0, 0)
+        scatter(0, 0)
+        copy_and_store(0, 0, 0)
+
+        for i, a in pairs[1:]:
+            fill(i, a)
+        for i, a in pairs[1:]:
+            scatter(i, a)
+        for n, (i, a) in enumerate(pairs):
+            if n > 0:
+                copy_and_store(n, i, a)

@@ -10,7 +10,7 @@ TOKENS = 512
 HALF = TOKENS // 2
 PIECE = 256
 PIECE_COLS = PIECE // 16
-WARM_UPS = 2
+WARM_UPS = 12
 FILL = 64
 
 FLOPS = 2 * P * (BLOCKS * P) * (SEQS * PIECE)
@@ -24,11 +24,11 @@ def tile_scatter_matmul_kernel(tc, base, x, w, offs, out):
         tc.tile_pool(name="held", bufs=1) as held,
         tc.psum_pool(name="banks", bufs=1) as banks,
     ):
-        zeros = held.tile([P, TOKENS], BF16, name="zeros")
+        zeros = held.tile([P, P], BF16, name="zeros")
         nc.vector.memset(zeros[:], 0.0)
-        unused = banks.tile([P, TOKENS], F32, name="unused")
+        unused = banks.tile([P, P], F32, name="unused")
         for n in range(WARM_UPS):
-            nc.tensor.matmul(unused[:], zeros[:, 0:P], zeros[:], start=True, stop=True)
+            nc.tensor.matmul(unused[:], zeros[:], zeros[:], start=True, stop=True)
 
         ident = held.tile([P, P], BF16, name="ident")
         make_identity(nc, ident[:])

@@ -43,13 +43,13 @@ def tile_scatter_matmul_kernel(tc, base, x, w, offs, out):
         w_tile = held.tile([P, BLOCKS * P], BF16, name="w_tile")
 
         nc.sync.dma_start(base_tiles[0, 0][:], base[0, 0:P, :])
-        nc.scalar.dma_start(w_tile[:], w)
+        nc.sync.dma_start(w_tile[:], w)
         nc.sync.dma_start(offsets[:], offs)
-        nc.scalar.dma_start(x_tiles[0][:], x[:, 0:PIECE])
+        nc.sync.dma_start(x_tiles[0][:], x[:, 0:PIECE])
         nc.sync.dma_start(base_tiles[0, 1][:], base[0, P : 2 * P, :])
-        nc.scalar.dma_start(base_tiles[1, 0][:], base[1, 0:P, :])
+        nc.sync.dma_start(base_tiles[1, 0][:], base[1, 0:P, :])
         nc.sync.dma_start(base_tiles[1, 1][:], base[1, P : 2 * P, :])
-        nc.scalar.dma_start(x_tiles[1][:], x[:, PIECE : 2 * PIECE])
+        nc.sync.dma_start(x_tiles[1][:], x[:, PIECE : 2 * PIECE])
 
         windows = {}
         for i, a in pairs:

@@ -11,7 +11,7 @@ HALF = TOKENS // 2
 PIECE = 256
 PIECE_COLS = PIECE // 16
 WARM_UPS = 12
-FILL = 64
+FILL = 44
 
 FLOPS = 2 * P * (BLOCKS * P) * (SEQS * PIECE)
 
@@ -43,10 +43,10 @@ def tile_scatter_matmul_kernel(tc, base, x, w, offs, out):
         w_tile = held.tile([P, BLOCKS * P], BF16, name="w_tile")
 
         nc.sync.dma_start(base_tiles[0, 0][:], base[0, 0:P, :])
+        nc.sync.dma_start(base_tiles[0, 1][:], base[0, P : 2 * P, :])
         nc.sync.dma_start(w_tile[:], w)
         nc.sync.dma_start(offsets[:], offs)
         nc.sync.dma_start(x_tiles[0][:], x[:, 0:PIECE])
-        nc.sync.dma_start(base_tiles[0, 1][:], base[0, P : 2 * P, :])
         nc.sync.dma_start(base_tiles[1, 0][:], base[1, 0:P, :])
         nc.sync.dma_start(base_tiles[1, 1][:], base[1, P : 2 * P, :])
         nc.sync.dma_start(x_tiles[1][:], x[:, PIECE : 2 * PIECE])
@@ -55,12 +55,13 @@ def tile_scatter_matmul_kernel(tc, base, x, w, offs, out):
         for i, a in pairs:
             windows[i, a] = banks.tile([P, TOKENS], F32, name="window_%d_%d" % (i, a))
 
-        def fill(i, a):
-            for c in range(0, TOKENS, FILL):
+        def fill(i, a, width):
+            for c in range(0, TOKENS, width):
+                cols = slice(c, min(c + width, TOKENS))
                 nc.tensor.matmul(
-                    windows[i, a][:, c : c + FILL],
+                    windows[i, a][:, cols],
                     ident[:],
-                    base_tiles[i, a][:, c : c + FILL],
+                    base_tiles[i, a][:, cols],
                     start=True,
                     stop=True,
                 )
@@ -85,14 +86,10 @@ def tile_scatter_matmul_kernel(tc, base, x, w, offs, out):
                     nc.scalar.copy(staged[:], windows[i, a][:, cols])
                     nc.scalar.dma_start(out[i, a * P : (a + 1) * P, cols], staged[:])
 
-        fill(0, 0)
-        scatter(0, 0)
-        copy_and_store(0, 0, 0)
-
-        for i, a in pairs[1:]:
-            fill(i, a)
-        for i, a in pairs[1:]:
-            scatter(i, a)
-        for n, (i, a) in enumerate(pairs):
-            if n > 0:
-                copy_and_store(n, i, a)
+        for i in range(SEQS):
+            for a in range(BLOCKS):
+                fill(i, a, TOKENS if i == 0 else FILL)
+            for a in range(BLOCKS):
+                scatter(i, a)
+            for a in range(BLOCKS):
+                copy_and_store(i * BLOCKS + a, i, a)

@@ -10,7 +10,9 @@ TOKENS = 512
 HALF = TOKENS // 2
 PIECE = 256
 PIECE_COLS = PIECE // 16
-WARM_UPS = 12
+THIN_ROUNDS = 2
+GROUP = 32
+WIDE = 6
 FILL = 44
 
 FLOPS = 2 * P * (BLOCKS * P) * (SEQS * PIECE)
@@ -27,7 +29,12 @@ def tile_scatter_matmul_kernel(tc, base, x, w, offs, out):
         zeros = held.tile([P, P], BF16, name="zeros")
         nc.vector.memset(zeros[:], 0.0)
         unused = banks.tile([P, P], F32, name="unused")
-        for n in range(WARM_UPS):
+        for n in range(THIN_ROUNDS):
+            for g in range(0, P, GROUP):
+                nc.tensor.matmul(
+                    unused[g : g + GROUP, :], zeros[:, 0:GROUP], zeros[:], start=True, stop=True
+                )
+        for n in range(WIDE):
             nc.tensor.matmul(unused[:], zeros[:], zeros[:], start=True, stop=True)
 
         ident = held.tile([P, P], BF16, name="ident")

import concourse.mybir as mybir
from concourse.masks import make_identity

BF16, F32, U16 = mybir.dt.bfloat16, mybir.dt.float32, mybir.dt.uint16

P = 128
SEQS = 2
BLOCKS = 2
TOKENS = 512
HALF = TOKENS // 2
PIECE = 256
PIECE_COLS = PIECE // 16
THIN_ROUNDS = 2
GROUP = 32
WIDE = 6
FILL = 44

FLOPS = 2 * P * (BLOCKS * P) * (SEQS * PIECE)


def tile_scatter_matmul_kernel(tc, base, x, w, offs, out):
    nc = tc.nc
    pairs = [(i, a) for i in range(SEQS) for a in range(BLOCKS)]

    with (
        tc.tile_pool(name="held", bufs=1) as held,
        tc.psum_pool(name="banks", bufs=1) as banks,
    ):
        zeros = held.tile([P, P], BF16, name="zeros")
        nc.vector.memset(zeros[:], 0.0)
        unused = banks.tile([P, P], F32, name="unused")
        for n in range(THIN_ROUNDS):
            for g in range(0, P, GROUP):
                nc.tensor.matmul(
                    unused[g : g + GROUP, :], zeros[:, 0:GROUP], zeros[:], start=True, stop=True
                )
        for n in range(WIDE):
            nc.tensor.matmul(unused[:], zeros[:], zeros[:], start=True, stop=True)

        ident = held.tile([P, P], BF16, name="ident")
        make_identity(nc, ident[:])

        base_tiles = {}
        x_tiles = {}
        for i, a in pairs:
            base_tiles[i, a] = held.tile([P, TOKENS], BF16, name="base_%d_%d" % (i, a))
        for i in range(SEQS):
            x_tiles[i] = held.tile([P, PIECE], BF16, name="x_%d" % i)
        offsets = held.tile([P, SEQS * PIECE_COLS], U16, name="offsets")
        w_tile = held.tile([P, BLOCKS * P], BF16, name="w_tile")

        nc.sync.dma_start(base_tiles[0, 0][:], base[0, 0:P, :])
        nc.sync.dma_start(base_tiles[0, 1][:], base[0, P : 2 * P, :])
        nc.sync.dma_start(w_tile[:], w)
        nc.sync.dma_start(offsets[:], offs)
        nc.sync.dma_start(x_tiles[0][:], x[:, 0:PIECE])
        nc.sync.dma_start(base_tiles[1, 0][:], base[1, 0:P, :])
        nc.sync.dma_start(base_tiles[1, 1][:], base[1, P : 2 * P, :])
        nc.sync.dma_start(x_tiles[1][:], x[:, PIECE : 2 * PIECE])

        windows = {}
        for i, a in pairs:
            windows[i, a] = banks.tile([P, TOKENS], F32, name="window_%d_%d" % (i, a))

        def fill(i, a, width):
            for c in range(0, TOKENS, width):
                cols = slice(c, min(c + width, TOKENS))
                nc.tensor.matmul(
                    windows[i, a][:, cols],
                    ident[:],
                    base_tiles[i, a][:, cols],
                    start=True,
                    stop=True,
                )

        def scatter(i, a):
            nc.tensor.matmul(
                windows[i, a][:].indirect(offsets[:, i * PIECE_COLS : (i + 1) * PIECE_COLS]),
                w_tile[:, a * P : (a + 1) * P],
                x_tiles[i][:],
                start=True,
                stop=True,
            )

        def copy_and_store(n, i, a):
            for h in range(2):
                cols = slice(h * HALF, (h + 1) * HALF)
                staged = held.tile([P, HALF], F32, name="staged_%d_%d_%d" % (i, a, h))
                if n % 2 == 0:
                    nc.vector.tensor_copy(staged[:], windows[i, a][:, cols])
                    nc.sync.dma_start(out[i, a * P : (a + 1) * P, cols], staged[:])
                else:
                    nc.scalar.copy(staged[:], windows[i, a][:, cols])
                    nc.scalar.dma_start(out[i, a * P : (a + 1) * P, cols], staged[:])

        for i in range(SEQS):
            for a in range(BLOCKS):
                fill(i, a, TOKENS if i == 0 else FILL)
            for a in range(BLOCKS):
                scatter(i, a)
            for a in range(BLOCKS):
                copy_and_store(i * BLOCKS + a, i, a)
